import numpy as np, ml_dtypes
CORES = [16,144,272,400]
N = 4
ROOT = 2
def setup_inputs(rng):
    return {"x": rng.standard_normal((N, 128, 8), dtype=np.float32).astype(ml_dtypes.bfloat16)}
def reference(x):
    y = np.full(x.shape, np.nan, x.dtype)
    y[ROOT] = x.max(axis=0)
    return {"y": y}

@@ -1,0 +1,53 @@
+import concourse.bass as bass
+
+SCRATCH = {
+    "mine": ("dram", [128, 8], "bfloat16"),
+    "in_a": ("dram", [128, 8], "bfloat16"),
+    "in_b": ("dram", [128, 8], "bfloat16"),
+}
+SEMAPHORES = ["local", "arrived", "result", "sent"]
+
+ENG = 0x1
+NENG = 1
+MAX = 2
+
+
+def rank_program(g, core, T, topo):
+    r0, r1, root, r3 = T.cores
+    helper = root + 1
+    sem = T.sem
+
+    def load():
+        g.dma_start(T.mine[:], T.x[:]).then_inc(sem.local, 16)
+        g.wait_ge(sem.local, 16)
+
+    def send(dst, out):
+        rid, pid = topo.addr(dst, core)
+        g.remote_dma(out[:], T.mine[:], sem.arrived, sem.sent, pid, rid, ENG)
+
+    def fold(dst, out, remote_sem):
+        rid, pid = topo.addr(dst, core)
+        return bass.RemoteDMATransfer(dst_ids=[bass.DstId(rid=rid, pnc=pid)], dma_engine_mask=ENG, remote_sem=remote_sem,
+                                      srcs=out[0], dsts=[out[1]], alu_op=MAX)
+
+    if core == r0 or core == r3:
+        load()
+        send(r1 if core == r0 else root, T.in_a)
+        g.wait_ge(sem.sent, NENG)
+    elif core == r1:
+        load()
+        g.wait_ge(sem.arrived, NENG)
+        g.remote_dma_fused([fold(helper, ([T.mine[:], T.in_a[:]], T.in_b[:]), sem.arrived)], local_sem=sem.sent)
+        g.wait_ge(sem.sent, NENG)
+    elif core == root:
+        load()
+        g.wait_ge(sem.arrived, NENG)
+        g.remote_dma_fused([fold(helper, ([T.mine[:], T.in_a[:]], T.in_a[:]), sem.arrived)], local_sem=sem.sent)
+        g.wait_ge(sem.result, NENG)
+        g.dma_start(T.y[:], T.in_b[:]).then_inc(sem.local, 16)
+        g.wait_ge(sem.local, 32)
+        g.wait_ge(sem.sent, NENG)
+    elif core == helper:
+        g.wait_ge(sem.arrived, 2 * NENG)
+        g.remote_dma_fused([fold(root, ([T.in_a[:], T.in_b[:]], T.in_b[:]), sem.result)], local_sem=sem.sent)
+        g.wait_ge(sem.sent, NENG)

@@ -7,8 +7,8 @@ SCRATCH = {
 }
 SEMAPHORES = ["local", "arrived", "result", "sent"]
 
-ENG = 0x1
-NENG = 1
+FAR = 8
+NEAR = 16
 MAX = 2
 
 
@@ -23,31 +23,32 @@ def rank_program(g, core, T, topo):
 
     def send(dst, out):
         rid, pid = topo.addr(dst, core)
-        g.remote_dma(out[:], T.mine[:], sem.arrived, sem.sent, pid, rid, ENG)
+        g.remote_dma(out[:], T.mine[:], sem.arrived, sem.sent, pid, rid, topo.mask(core, dst))
 
-    def fold(dst, out, remote_sem):
+    def fold(dst, srcs, out, remote_sem):
         rid, pid = topo.addr(dst, core)
-        return bass.RemoteDMATransfer(dst_ids=[bass.DstId(rid=rid, pnc=pid)], dma_engine_mask=ENG, remote_sem=remote_sem,
-                                      srcs=out[0], dsts=[out[1]], alu_op=MAX)
+        t = bass.RemoteDMATransfer(dst_ids=[bass.DstId(rid=rid, pnc=pid)], dma_engine_mask=topo.mask(core, dst),
+                                   remote_sem=remote_sem, srcs=srcs, dsts=[out], alu_op=MAX)
+        g.remote_dma_fused([t], local_sem=sem.sent)
 
     if core == r0 or core == r3:
         load()
         send(r1 if core == r0 else root, T.in_a)
-        g.wait_ge(sem.sent, NENG)
+        g.wait_ge(sem.sent, FAR)
     elif core == r1:
         load()
-        g.wait_ge(sem.arrived, NENG)
-        g.remote_dma_fused([fold(helper, ([T.mine[:], T.in_a[:]], T.in_b[:]), sem.arrived)], local_sem=sem.sent)
-        g.wait_ge(sem.sent, NENG)
+        g.wait_ge(sem.arrived, FAR)
+        fold(helper, [T.mine[:], T.in_a[:]], T.in_b[:], sem.arrived)
+        g.wait_ge(sem.sent, FAR)
     elif core == root:
         load()
-        g.wait_ge(sem.arrived, NENG)
-        g.remote_dma_fused([fold(helper, ([T.mine[:], T.in_a[:]], T.in_a[:]), sem.arrived)], local_sem=sem.sent)
-        g.wait_ge(sem.result, NENG)
+        g.wait_ge(sem.arrived, FAR)
+        fold(helper, [T.mine[:], T.in_a[:]], T.in_a[:], sem.arrived)
+        g.wait_ge(sem.result, NEAR)
         g.dma_start(T.y[:], T.in_b[:]).then_inc(sem.local, 16)
         g.wait_ge(sem.local, 32)
-        g.wait_ge(sem.sent, NENG)
+        g.wait_ge(sem.sent, NEAR)
     elif core == helper:
-        g.wait_ge(sem.arrived, 2 * NENG)
-        g.remote_dma_fused([fold(root, ([T.in_a[:], T.in_b[:]], T.in_b[:]), sem.result)], local_sem=sem.sent)
-        g.wait_ge(sem.sent, NENG)
+        g.wait_ge(sem.arrived, FAR + NEAR)
+        fold(root, [T.in_a[:], T.in_b[:]], T.in_b[:], sem.result)
+        g.wait_ge(sem.sent, NEAR)

import concourse.bass as bass

SCRATCH = {
    "mine": ("dram", [128, 8], "bfloat16"),
    "in_a": ("dram", [128, 8], "bfloat16"),
    "in_b": ("dram", [128, 8], "bfloat16"),
}
SEMAPHORES = ["local", "arrived", "result", "sent"]

FAR = 8
NEAR = 16
MAX = 2


def rank_program(g, core, T, topo):
    r0, r1, root, r3 = T.cores
    helper = root + 1
    sem = T.sem

    def load():
        g.dma_start(T.mine[:], T.x[:]).then_inc(sem.local, 16)
        g.wait_ge(sem.local, 16)

    def send(dst, out):
        rid, pid = topo.addr(dst, core)
        g.remote_dma(out[:], T.mine[:], sem.arrived, sem.sent, pid, rid, topo.mask(core, dst))

    def fold(dst, srcs, out, remote_sem):
        rid, pid = topo.addr(dst, core)
        t = bass.RemoteDMATransfer(dst_ids=[bass.DstId(rid=rid, pnc=pid)], dma_engine_mask=topo.mask(core, dst),
                                   remote_sem=remote_sem, srcs=srcs, dsts=[out], alu_op=MAX)
        g.remote_dma_fused([t], local_sem=sem.sent)

    if core == r0 or core == r3:
        load()
        send(r1 if core == r0 else root, T.in_a)
        g.wait_ge(sem.sent, FAR)
    elif core == r1:
        load()
        g.wait_ge(sem.arrived, FAR)
        fold(helper, [T.mine[:], T.in_a[:]], T.in_b[:], sem.arrived)
        g.wait_ge(sem.sent, FAR)
    elif core == root:
        load()
        g.wait_ge(sem.arrived, FAR)
        fold(helper, [T.mine[:], T.in_a[:]], T.in_a[:], sem.arrived)
        g.wait_ge(sem.result, NEAR)
        g.dma_start(T.y[:], T.in_b[:]).then_inc(sem.local, 16)
        g.wait_ge(sem.local, 32)
        g.wait_ge(sem.sent, NEAR)
    elif core == helper:
        g.wait_ge(sem.arrived, FAR + NEAR)
        fold(root, [T.in_a[:], T.in_b[:]], T.in_b[:], sem.result)
        g.wait_ge(sem.sent, NEAR)
